import numpy as np, ml_dtypes
CORES = [9,25,41,57]
N = 4
BF = ml_dtypes.bfloat16
def gentries(a):
    return np.ascontiguousarray(a.reshape(8, 16, -1).transpose(0, 2, 1)).reshape(8, -1)
def gtable(e):
    e = np.asarray(e); return np.ascontiguousarray(e.reshape(8, -1, 16).transpose(0, 2, 1)).reshape(128, -1).astype(np.int32)
K, C, NS, RO = 256, 4, 896, 6
V, W = C * K, N * C * K
def parts(rng):
    lev = rng.integers(0, 160, (N, 8, 1, W)); b = lev + ((256 - lev) * rng.random((N, 8, 16, W))).astype(np.int64)
    L = rng.integers(0, W, (N, 8, 16, NS)); S = rng.integers(0, W, (N, 8, 16, V))
    P = np.argsort(rng.random((N, 8, C, NS)), axis=-1)[..., :K].reshape(N, 8, V); Q = rng.integers(0, NS, (N, 8, V))
    return np.minimum(b, 255), L, S, P, Q, rng.integers(400, 2000, (N, 8, 16, 1)), rng.integers(1600, 2900, (N, 8, 1))
def pack(b, L, S, P, Q, th, mg):
    return {"base": np.ascontiguousarray(b.reshape(N, 128, W)).astype(np.float32).astype(BF), "favor": np.ascontiguousarray(L.reshape(N, 128, NS)).astype(np.int32),
            "src": np.ascontiguousarray(S.reshape(N, 128, V)).astype(np.int32), "grant": np.stack([gtable(a) for a in P]), "part": np.stack([gtable(a) for a in Q]),
            "th": np.ascontiguousarray(th.reshape(N, 128, 1)).astype(np.int32), "mg": mg.astype(np.int32)}
def setup_inputs(rng):
    return pack(*parts(rng))
def setup_inputs_spread(rng):
    b, L, S, P, Q, th, mg = parts(rng)
    b = np.minimum((256 * rng.random((N, 8, 16, W)) * np.exp2(-rng.integers(0, 8, (N, 8, 1, W)).astype(np.float64))).astype(np.int64), 255)
    L = np.minimum((W * rng.random(L.shape) ** 3).astype(np.int64), W - 1); S = np.minimum((W * rng.random(S.shape) ** 2).astype(np.int64), W - 1)
    Q = np.minimum((NS * rng.random(Q.shape) ** 3).astype(np.int64), NS - 1)
    th = np.minimum(np.exp2(12 * rng.random(th.shape)).astype(np.int64) - 1, 4079); mg = np.minimum(np.exp2(12 * rng.random(mg.shape)).astype(np.int64) - 1, 4079)
    return pack(b, L, S, P, Q, th, mg)
def setup_inputs_ends(rng):
    b, L, S, P, Q, th, mg = parts(rng)
    def tip(x, lo, hi, share):
        m = rng.random(x.shape); return np.where(m < 0.5 * share, lo, np.where(m < share, hi, x))
    sort_ = rng.integers(0, 5, (N, 8, 1, W)); el = 255 * rng.integers(0, 2, b.shape)
    b = np.where(sort_ == 0, 0, np.where(sort_ == 1, 255, np.where(sort_ < 4, el, tip(b, 0, 255, 0.5))))
    L = tip(L, 0, W - 1, 0.7); S = tip(S, 0, W - 1, 0.7); Q = tip(Q, 0, NS - 1, 0.8)
    ix = np.concatenate([np.arange(K // 2), np.arange(NS - K // 2, NS)]); P = rng.permuted(np.tile(ix, (N, 8, C, 1)), axis=-1).reshape(N, 8, V)
    th = tip(th, 0, 4079, 1.0); th[:, :, 15] = 4079; th[:, :, 0] = 0
    for r in range(N):
        last = 4079 if (N - 1 - r) % 2 == 0 else 0
        mg[r, :7, 0] = rng.permutation(np.array([0, 0, 0, 4079, 4079, 4079, 4079 - last])); mg[r, 7, 0] = last
    zero = rng.random((N, 8)) < 0.7; zero[:, 7] = True
    b[..., W - 1] = np.where(zero[:, :, None], 0, b[..., W - 1])
    hi = np.array([0, K + 1, K - 2, 2 * K - 1, V - 1, V - 2 - K]); lo = np.array([K, 1, 2 * K - 2, K - 1, V - 2, V - 1 - K])
    b[:, :, :, hi] = 255; b[:, :, :, lo] = 0; S[:, :, 15, hi] = W - 1; S[:, :, 15, lo] = 0
    np.put_along_axis(L[:, :, 15], P[:, :, hi], W - 1, 2)
    return pack(b, L, S, P, Q, th, mg)
def setup_inputs_corners(rng):
    b, L, S, P, Q, th, mg = parts(rng); e = np.arange(V); rev = (e // K ^ 1) * K + e % K
    for r in range(N):
        for g, k in enumerate(rng.permutation(8)):
            if k == 0: S[r, g] = e
            if k == 1:
                L[r, g] = rng.integers(0, W, (1, NS)); S[r, g] = rng.choice(np.array([0, V - 1, V, W - 1]), (16, V)); Q[r, g] = rng.choice(np.array([0, NS - 1]), V)
            if k == 2:
                b[r, g] = rng.integers(0, 4, (16, W)); th[r, g, :, 0] = rng.integers(0, 41, 16); mg[r, g, 0] = rng.integers(0, 21)
            if k == 3:
                Q[r, g] = P[r, g]; S[r, g] = rev; mg[r, g, 0] = rng.integers(0, 600)
                for c in range(C):
                    a = e[c * K:(c + 1) * K]; L[r, g][:, P[r, g, a]] = np.where(rng.random((16, K)) < 0.5, a, rev[a])
            if k == 4:
                L[r, g] = rng.integers(V, W, (16, NS)); S[r, g] = rng.integers(V, W, (16, V)); th[r, g] = 4079; mg[r, g] = 4079
            if k == 5: th[r, g] = 0; mg[r, g] = 0
            if k == 6:
                b[r, g] = 255 * rng.integers(0, 2, (16, W)); L[r, g, 8:] = L[r, g, :8]; th[r, g, :, 0] = 255 * rng.integers(0, 16, 16); mg[r, g, 0] = 255 * rng.integers(0, 9)
            if k == 7:
                b[r, g] = 8 * rng.integers(0, 32, (1, W)); th[r, g, :, 0] = 128 * rng.integers(1, 20, 16); mg[r, g, 0] = 128 * rng.integers(4, 14)
    return pack(b, L, S, P, Q, th, mg)
def setup_inputs_crowd(rng):
    b, L, S, P, Q, th, mg = parts(rng); z = (1 + (RO - 1) % (N - 1)) * V + ((RO - 1) % C) * K
    s = 490 + np.arange(64); low = (s // 16)[None, :] + (np.arange(16)[:, None] < (s % 16)[None, :]).astype(np.int64)
    for r in range(N):
        for g, k in enumerate(rng.permutation(8) % 4):
            if k == 3: continue
            b[r, g, :, :V] = rng.integers(200, 256, (16, V)); b[r, g, :, z:z + 64] = low; b[r, g, :, z + 64:z + K] = 0
            L[r, g] = z + K - 1 if k == 2 else rng.integers(z + 64, z + K, (16, NS))
            if k == 2: Q[r, g] = rng.integers(0, NS)
            c0 = (1, 0, C - 1)[k]; a = int(rng.integers(0, K)) + K * np.arange(c0, C)
            b[r, g][:, a] = 0; S[r, g][:, a] = z + rng.integers(0, 64, (16, C - c0))
            th[r, g, :, 0] = rng.integers(480, 521, 16); mg[r, g, 0] = rng.choice(np.array([0, 1, 3199]))
    return pack(b, L, S, P, Q, th, mg)
def check_inputs(d):
    bad = []; x = np.asarray(d["base"]).astype(np.float32)
    if not np.all((x >= 0) & (x <= 255) & (x == np.floor(x))): bad.append("range of base")
    for k, lo, hi in (("favor", 0, W - 1), ("src", 0, W - 1), ("grant", 0, NS - 1), ("part", 0, NS - 1), ("th", 0, 4079), ("mg", 0, 4079)):
        if np.min(d[k]) < lo or np.max(d[k]) > hi: bad.append("range of " + k)
    p = np.sort(np.stack([gentries(a) for a in d["grant"]]).astype(np.int64).reshape(N, 8, C, K), axis=-1)
    if np.any(p[..., 1:] == p[..., :-1]): bad.append("grantors of a class differ")
    return bad
def reference(base, favor, src, grant, part, th, mg):
    b = base.astype(np.float32).astype(np.int64).reshape(N, 8, 16, W); X = b + 0
    L = favor.astype(np.int64).reshape(N, 8, 16, NS); S = src.astype(np.int64).reshape(N, 8, 16, V)
    P = np.stack([gentries(a) for a in grant]).astype(np.int64); Q = np.stack([gentries(a) for a in part]).astype(np.int64)
    lim = th.astype(np.int64).reshape(N, 8, 16, 1); gap = mg.astype(np.int64).reshape(N, 8, 1); A = np.zeros((N, 8), np.int64); lane = np.arange(K)
    for t in range(RO):
        c = t % C; o = c * K; v = (c ^ 1) * K; e = o + lane; be = b[..., o:o + K]; old = X[..., o:o + K] + 0; s = S[..., o:o + K] + 0
        far = np.take_along_axis(X, s.reshape(N, 8, 1, 16 * K), 3).reshape(N, 8, 16, 16, K)
        dist = np.sum(np.abs(far - old[:, :, :, None, :]), axis=2)
        lapse = dist > lim + (A & 31)[:, :, None, None]
        x = np.where(lapse, be, old); s = np.where(lapse, e, s)
        pe = P[:, :, None, o:o + K]; T = np.take_along_axis(L, pe, 3)
        y = np.take_along_axis(X, T.reshape(N, 8, 1, 16 * K), 3).reshape(N, 8, 16, 16, K)
        k1 = np.argmin(y, axis=3); least = np.min(y, axis=3); less = least < x
        x = np.where(less, least, x); s = np.where(less, np.take_along_axis(T, k1, 2), s)
        den = np.sum(be - x, axis=2) - np.sum(b[..., v:v + K] - X[..., v:v + K], axis=2) > gap
        k2 = np.sum(y[:, :, :, 0, :], axis=2) & 15
        new = np.take_along_axis(np.take_along_axis(L, Q[:, :, None, o:o + K], 3), k2[:, :, None, :], 2)
        put = den[:, :, None, :] & (np.arange(16)[:, None] == ((lane + t) & 15)[None, :])
        np.put_along_axis(L, np.broadcast_to(pe, T.shape), np.where(put, new, T), 3)
        x = np.where(den[:, :, None, :], be, x); s = np.where(den[:, :, None, :], e, s); A = A + np.sum(den, axis=2)
        d = 1 + t % (N - 1)
        X[..., o:o + K] = x; S[..., o:o + K] = s; X[..., d * V + o:d * V + o + K] = np.roll(x, d, axis=0)
    return {"yx": X.reshape(N, 128, W).astype(np.float32).astype(BF), "ys": S.reshape(N, 128, V).astype(np.float32), "yl": L.reshape(N, 128, NS).astype(np.float32)}

from concourse.mybir import AluOpType as A, ActivationFunctionType as AF
import comms_topo

K, W, V, NS, RO = 256, 4096, 1024, 896, 6
EARLY = (("S", 0, 80), ("S", 80, 160), ("S", 160, 224), ("S", 224, 256))
LATE = (("V", 0, 80), ("S", 80, 144), ("S", 144, 192), ("V", 192, 208), ("S", 208, 256))
EBG = (3, 2, 2, 1, 9)
LBG = (3, 0, 3, 3, 9, 9)
CW = 80 * 16
BF, F3, I3, U1 = "bfloat16", "float32", "int32", "uint16"
BANKS = ("pB", "pV", "pD", "pK", "pO", "pH", "pJ", "pX")
_B = {"gr": (64, I3), "pa": (64, I3), "P16": (64, U1), "Q16": (64, U1), "fav": (NS, I3), "Lf": (NS, F3), "Bb": (V, BF),
      "Si": (V, I3), "S16": (V, U1), "T16": (K, U1), "ysf": (V, F3), "D0": (CW, BF), "RI": (272, BF), "THR": (272, BF),
      "JR": (512, BF), "JL": (1024, BF), "LE": (512, BF)}
for _d, _w, _l in ((BF, W, "Xb F0 F1 F2 M0 M1 M2"), (F3, W, "Z Y SCN"), (I3, K, "mi hi h15 s2"),
                   (F3, K, "Tf Fm0 Fm1 y0a mask mLQ w q s1"),
                   (BF, K, "mx x1_0 x1_1 sgd0 sgd1 sgl0 sgl1 t0 x04 x05 y0b ones"),
                   (BF, K, " ".join("xs%d land%d" % (_t, _t) for _t in range(RO))),
                   (I3, 1, "thc mg8 as0 as1 a63 ki ki2 mgi mq ml"),
                   (F3, 1, "mgf acc lim0 lim1 lim2 nth kcf mqa mqb mlf ca cb cc ckA ckB"),
                   (BF, 128, "Ib tb Blk Bp Bn Bneg I5 I14 I22 I12 I256 KC BC MgA MgB"), (BF, 144, "Gm G2 Gn"),
                   (F3, 128, "If Imf Blkf R8 R8a onf")):
    for _n in _l.split():
        _B[_n] = (_w, _d)
SCRATCH = {n: ("sbuf", [128, w], d) for n, (w, d) in _B.items()}
for _n in BANKS:
    SCRATCH[_n] = ("psum", [128, 512], F3)
SEMAPHORES = ["eV", "eS", "eP", "eG"] + ["d%d" % i for i in range(40)] + ["arr%d" % i for i in range(RO)] + ["loc%d" % i for i in range(RO)]


def rank_program(g, core, T, topo):
    rank = T.rank_of(core)
    if rank is None:
        return
    N = len(T.cores)
    queue = {"V": g.vector, "S": g.scalar, "P": g.tensor, "G": g, "Y": g.sync}
    count = {"eV": 0, "eS": 0, "eP": 0, "eG": 0}
    clk = {q: {} for q in queue}
    hist = {}
    ndma = [0]

    def at(name, c0=0, c1=None, step=None, r0=0, r1=128):
        c1 = (512 if name in BANKS else _B[name][0]) if c1 is None else c1
        ap = T[name][r0:r1, c0:c1] if step is None else T[name][r0:r1, c0:c1:step]
        return (ap, name, c0, c1)

    def waits(q, me, ins, outs):
        cand = {}
        for wr, regs in ((False, ins), (True, outs)):
            for (_, name, lo, hi) in regs:
                for rlo, rhi, rw, rme, rsem, rn, rclk in hist.get(name, ()):
                    if rme == me and me == "P":
                        continue
                    if not (lo < rhi and rlo < hi and (wr or rw)) and (rme == me or name not in BANKS):
                        continue
                    if clk[q].get(rsem, 0) < rn and (rsem not in cand or cand[rsem][0] < rn):
                        cand[rsem] = (rn, rclk)
        for s in list(cand):
            n = cand[s][0]
            if not any(o != s and cand[o][1].get(s, 0) >= n for o in cand):
                queue[q].wait_ge(T.sem[s], n)
        for s, (n, rc) in cand.items():
            for a, b in list(rc.items()) + [(s, n)]:
                clk[q][a] = max(clk[q].get(a, 0), b)

    def note(q, me, sem, n, ins, outs):
        count[sem] = n
        snap = dict(clk[q]) if q else {}
        snap[sem] = n
        for w, regs in ((True, outs), (False, ins)):
            for (_, name, lo, hi) in regs:
                keep = [r for r in hist.get(name, ()) if not (lo <= r[0] and r[1] <= hi and (w or (r[3] == me and not r[2])))]
                hist[name] = keep + [(lo, hi, w, me, sem, n, snap)]

    def emit(q, f, outs, ins):
        if q == "G":
            outs = outs + [(None, "gq", 0, 1)]
        waits(q, q, ins, outs)
        f().then_inc(T.sem["e" + q], 1)
        note(q, q, "e" + q, count["e" + q] + 1, ins, outs)

    def dma(q, out, in_):
        outs = [out] if isinstance(out, tuple) else []
        ins = [in_] if isinstance(in_, tuple) else []
        s = "d%d" % ndma[0]
        ndma[0] += 1
        waits(q, s, ins, outs)
        queue[q].dma_start(out[0] if outs else out, in_[0] if ins else in_).then_inc(T.sem[s], 16)
        note(q, s, s, 16, ins, outs)

    def tt(out, a, b, op):
        emit("V", lambda: g.vector.tensor_tensor(out=out[0], in0=a[0], in1=b[0], op=op), [out], [a, b])

    def ts(out, a, s1, s2, op0, op1=None):
        ins = [a] + [s for s in (s1, s2) if isinstance(s, tuple)]
        v1 = s1[0] if isinstance(s1, tuple) else s1
        v2 = s2[0] if isinstance(s2, tuple) else s2
        kw = {} if op1 is None else {"op1": op1}
        emit("V", lambda: g.vector.tensor_scalar(out=out[0], in0=a[0], scalar1=v1, scalar2=v2, op0=op0, **kw), [out], ins)

    def cp(out, a):
        emit("V", lambda: g.vector.tensor_copy(out=out[0], in_=a[0]), [out], [a])

    def ms(out, c):
        emit("V", lambda: g.vector.memset(out[0], c), [out], [])

    def act(out, a, func=AF.Identity, bias=0.0, scale=1.0, accum=None):
        ins = [a] + ([bias] if isinstance(bias, tuple) else [])
        kw = {} if accum is None else {"accum_out": accum[0]}
        b = bias[0] if isinstance(bias, tuple) else bias
        emit("S", lambda: g.scalar.activation(out=out[0], in_=a[0], func=func, bias=b, scale=scale, **kw), [out] + ([accum] if accum else []), ins)

    def mm(out, l, r, start, stop):
        emit("P", lambda: g.tensor.matmul(out=out[0], lhsT=l[0], rhs=r[0], start=start, stop=stop), [out], [l, r])

    def group(out, pairs):
        for i, (l, r) in enumerate(pairs):
            mm(out, l, r, i == 0, i == len(pairs) - 1)

    def gather(q, out, win, off):
        if q == "S":
            emit("S", lambda: g.scalar.activation(out=out[0], in_=win[0].indirect(off[0]), func=AF.Copy), [out], [win, off])
        else:
            emit("V", lambda: g.vector.tensor_copy(out=out[0], in_=win[0].indirect(off[0])), [out], [win, off])

    dma("Y", at("gr"), T.grant[:])
    dma("S", at("fav"), T.favor[:])
    for i in range(4):
        dma("Y", at("Xb", 1024 * i, 1024 * i + 1024), T.base[:, 1024 * i:1024 * i + 1024])
    dma("S", at("mg8", r1=8), T.mg[:])
    dma("S", at("thc"), T.th[:])
    dma("S", at("pa"), T.part[:])
    dma("S", at("Si"), T.src[:])
    dma("Y", at("Bb"), T.base[:, 0:V])

    def iota(out, pattern, base, cm=0, **kw):
        emit("G", lambda: g.iota(out[0], pattern, base, cm, **kw), [out], [])

    def select(out, a, pattern, op, base, cm):
        emit("G", lambda: g.affine_select(out[0], a[0], pattern, op, 0.0, base, cm), [out], [a])
    small = dict(allow_small_or_imprecise_dtypes=True)
    ms(at("onf", r1=8), 1.0)
    ms(at("ones"), 1.0)
    ms(at("JR"), 0.0)
    select(at("Ib"), at("ones", 0, 128), [[-1, 128]], A.is_equal, 0, 1)
    iota(at("JR", r0=32, r1=33), [[0, 32], [1, 16]], 0, **small)
    iota(at("JR", r1=1), [[16, 32], [0, 16]], 0, **small)
    ms(at("JL", r1=64), 2.0 ** -16)
    ms(at("JL", r0=64), -128.0)
    ts(at("JR", r0=32, r1=33), at("JR", r0=32, r1=33), 0.5, None, A.add)
    ms(at("JR", r0=64, r1=65), 2.0 ** -7)
    ms(at("JR", r0=96, r1=97), 1.0)
    iota(at("JL", r0=64, r1=65), [[1, 8], [0, 128]], 120, **small)
    select(at("tb"), at("ones", 0, 128), [[-16, 8], [0, 16]], A.is_ge, 0, 1)
    select(at("Blk"), at("tb"), [[16, 8], [0, 16]], A.is_ge, 15, -1)
    iota(at("ki"), [[0, 1]], 0, 1)
    select(at("R8a", r1=8), at("onf", r1=8), [[1, 128]], A.is_ge, 0, -16)
    select(at("R8", r1=8), at("R8a", r1=8), [[-1, 128]], A.is_ge, 15, 16)
    iota(at("RI"), [[0, 17], [1, 16]], 0, **small)
    for b in range(8):
        mm(at(BANKS[b]), at("JL", 128 * b, 128 * b + 128), at("JR"), True, b % 2 == 0)
    cp(at("P16"), at("gr"))
    cp(at("Lf"), at("fav"))

    def tgather(t):
        c = t % 4
        gather("V", at("T16"), at("Lf"), at("P16", 16 * c, 16 * c + 16))
    tgather(0)
    ms(at("D0"), -1.0 / 16)
    ms(at("D0", 0, CW, 16), 512.0)
    ms(at("BC", r1=64), 0.0)
    ms(at("BC", r0=64), 0.0)
    ms(at("BC", r0=96), -128.0)
    ts(at("ki2"), at("ki"), 15, None, A.bitwise_and)
    cp(at("kcf"), at("ki2"))
    ts(at("THR"), at("RI"), at("kcf"), 2.0 ** 30, A.not_equal, A.mult)
    cp(at("mgf", r1=8), at("mg8", r1=8))
    for n, m, v in (("Bp", "Blk", 8192.0), ("Bn", "Blk", -8192.0), ("Blkf", "Blk", 1.0), ("Imf", "Ib", -1.0), ("Bneg", "Blk", -1.0), ("If", "Ib", 65536.0),
                    ("I5", "Ib", -81920.0), ("I14", "Ib", 16384.0), ("I22", "Ib", -4194304.0), ("I12", "Ib", 4096.0), ("I256", "Ib", 256.0)):
        act(at(n), at(m), AF.Copy, scale=v)
    for b in range(8):
        x = at("Xb", 512 * b, 512 * b + 512)
        if b % 2 == 0:
            tt(at("Z", 512 * b, 512 * b + 512), x, at(BANKS[b]), A.add)
        else:
            mm(at(BANKS[b]), at("Ib"), x, False, True)
            act(at("Z", 512 * b, 512 * b + 512), at(BANKS[b]), AF.Copy)

    def consts1():
        cp(at("Q16"), at("pa"))
        mm(at("pX", 0, 1), at("R8", r1=8), at("mgf", r1=8), True, True)
        cp(at("mgi"), at("pX", 0, 1))
        ts(at("mq"), at("mgi"), 5, None, A.arith_shift_right)
        ts(at("ml"), at("mgi"), 31, None, A.bitwise_and)
        ts(at("mqa"), at("mq"), 64.0, -8192.0 * 32, A.add, A.mult)
        ts(at("mqb"), at("mq"), -8192.0 * 32, None, A.mult)
        ts(at("mlf"), at("ml"), 0.5, -8192.0, A.add, A.mult)
        ts(at("ca"), at("kcf"), 0.0, at("mqa"), A.is_equal, A.mult)
        ts(at("cb"), at("kcf"), 0.0, at("mqb"), A.is_equal, A.mult)
        ts(at("cc"), at("kcf"), 1.0, at("mlf"), A.is_equal, A.mult)
        tt(at("ckA"), at("ca"), at("cc"), A.add)
        tt(at("ckB"), at("cb"), at("cc"), A.add)
        ts(at("MgA"), at("Blk"), at("ckA"), None, A.mult)
        ts(at("MgB"), at("Blk"), at("ckB"), None, A.mult)

    def consts2():
        ms(at("Gm"), 0.0)
        cp(at("Gm", 15, 128, 16), at("Blk", 0, 128, 16))
        ts(at("G2"), at("Gm"), 2.0, None, A.mult)
        ts(at("Gn"), at("Gm"), -1.0, None, A.mult)
        ms(at("LE", r1=64), 1.0)
        for c in range(4):
            ms(at("LE", 128 * c, 128 * c + 128, r0=64), 32768.0 * (16 + c))
        ms(at("LE", r0=96), -0.5)
        ms(at("KC", r1=64), 0.0)
        ms(at("KC", r0=64), -6291456.0 * 128)
        ms(at("KC", r0=96), -0.5)
        ts(at("nth"), at("thc"), -1.0, -0.5, A.mult, A.add)
        cp(at("lim0"), at("nth"))
        ms(at("as0"), 0)
        for c in range(1, 4):
            cp(at("S16", c * K, c * K + K), at("Si", c * K, c * K + K))

    def cls(t):
        return t % 4, t % 4 * K

    def told(t):
        return (1 + t % (N - 1)) * V + t % 4 * K

    def bcol(c):
        return at("Bb", c * K, c * K + K)

    def pre(t):
        c, o = cls(t)
        group(at("pB", 0, K), [(at("Ib"), bcol(c)), (at("BC"), at("JR", 0, K))])
        u = [r for r in range(t) if r % 4 == c ^ 1]
        mm(at("pV", 0, K), at("Bp"), bcol(c), True, False)
        mm(at("pV", 0, K), at("MgB" if u else "MgA"), at("ones"), False, False)
        if u:
            mm(at("pV", 0, K), at("Bn"), bcol(c ^ 1), False, False)
            mm(at("pV", 0, K), at("Bp"), at("xs%d" % u[-1]), False, False)
        if t < RO - 1:
            for h, n in ((0, o), (K, told(t))):
                b, s = n // 512, n % 512
                mm(at("pJ", h, h + K), at("JL", 128 * b, 128 * b + 128, r1=96), at("JR", s, s + K, r1=96), True, True)

    def x0col(t):
        return at("pB", 0, K) if t < 4 else at("pB", K, 2 * K)

    def fargather(t, h):
        o, h = t % 4 * K, h * 128
        gather("S", at("F%d" % (t % 3), 16 * h, 16 * h + 2048), at("Xb"), at("S16", o + h, o + h + 128))

    def farstart(t):
        c, o = cls(t)
        old = bcol(c) if t < 4 else at("Xb", o, o + K)
        for h in (0, 1):
            mm(at("pO", h, 512, 2), at("Ib"), old, True, True)
        mm(at("pD", 0, K), at("Bneg"), old, True, False)
        for p in range(16):
            mm(at("pD", 0, K), at("Gn", 15 - p, 143 - p), at("F%d" % (t % 3), p, W, 16), False, False)

    def farops(t):
        f, m = "F%d" % (t % 3), "M%d" % (t % 3)

        def one(p):
            tt(at(m, 512 * p, 512 * p + 512), at(f, p, W, 8), at("pO"), A.max)
            for h in (0, 1):
                mm(at("pD", 0, K), at("G2", 15 - p - 8 * h, 143 - p - 8 * h), at(m, 512 * p + h, 512 * p + 512, 2), False, p == 7 and h == 1)
        return [lambda p=p: one(p) for p in range(8)]

    def sgnl(t):
        act(at("sgl%d" % (t % 2)), at("pD", 0, K), AF.Sign, bias=at("lim%d" % (t % 3)))

    def limits(t):
        a, b = "as%d" % ((t - 1) % 2), "as%d" % (t % 2)
        tt(at(b), at(a), at("acc"), A.add)
        ts(at("a63"), at(b), 63, None, A.bitwise_and)
        ts(at("lim%d" % (t % 3)), at("a63"), -0.5, at("nth"), A.mult, A.add)

    def sgnd(t):
        act(at("sgd%d" % (t % 2)), at("pV", 0, K), AF.Sign, accum=at("acc"))

    def lapse_x(t):
        c, o = cls(t)
        mm(at("pO", 0, K), at("I256"), at("sgl%d" % (t % 2)), True, True)
        mm(at("pO", K, 2 * K), at("Ib"), bcol(c), True, True)
        tt(at("t0"), at("Xb", o, o + K), at("pO", 0, K), A.max)
        tt(at("x0%d" % t), at("t0"), at("pO", K, 2 * K), A.min)
        group(at("pB", K, 2 * K), [(at("Ib"), at("x0%d" % t)), (at("BC"), at("JR", 0, K))])

    def xbput(n, x):
        act(at("Xb", n, n + K), at(x), AF.Identity, bias=128.0)

    def schain_pe(t):
        c, o = cls(t)
        x0 = bcol(c) if t < 4 else at("x0%d" % t)
        sd, sl = at("sgd%d" % (t % 2)), at("sgl%d" % (t % 2))
        group(at("pK", K, 2 * K), [(at("LE", 128 * c, 128 * c + 128), at("JR", 0, K)), (at("I12"), sl), (at("I12"), sd)])
        group(at("pK", 0, K), [(at("If"), at("Fm%d" % (t % 2))), (at("I5"), at("x1_%d" % (t % 2))), (at("I14"), x0), (at("KC"), at("JR", 0, K)), (at("I22"), sd)])

    def schain_v(t):
        c, o = cls(t)
        blk = at("Si", o, o + K)
        tt(at("s1"), blk, at("pK", K, 2 * K), A.max)
        tt(at("s2"), at("s1"), at("pK", 0, K), A.max)
        ts(blk, at("s2"), 4095, None, A.bitwise_and)
        cp(at("S16" if t < 2 else "ysf", o, o + K), blk)
        if t >= 2:
            dma("Y", T.ys[:, o:o + K], at("ysf", o, o + K))

    bg = []

    def run_bg(k):
        for _ in range(k):
            if bg:
                bg.pop(0)()

    for t in range(RO):
        c, o = cls(t)
        late = t >= 4
        if t >= 1:
            pre(t)
            limits(t)
        if late:
            fargather(t, 0)
            fargather(t, 1)
        for ci, (q, a, b) in enumerate(LATE if late else EARLY):
            y, d0, sc = at("Y", 16 * a, 16 * b), at("D0", 0, 16 * (b - a)), at("SCN", 16 * a, 16 * b)
            gather(q, y, at("Z"), at("T16", a, b))
            if t == 0 and ci == 0:
                consts1()
                pre(0)
                cp(at("S16", 0, K), at("Si", 0, K))
            if not late and ci == 0:
                run_bg(EBG[0])
            if late and ci == 1:
                if t == 4:
                    farstart(3)
                    bg.extend(farops(3))
                    run_bg(99)
                    sgnl(3)
                else:
                    schain_pe(4)
                    schain_v(4)
                farstart(t)
                bg.extend(farops(t))
                run_bg(LBG[0])
            if t == 4 and ci == 4:
                schain_pe(3)
                schain_v(3)
            emit("V", lambda: g.vector.tensor_tensor_scan(out=sc[0], data0=d0[0], data1=y[0], initial=512.0, op0=A.add, op1=A.min), [sc], [d0, y])
            run_bg((LBG if late else EBG)[ci + 1])
        run_bg(99)
        if late:
            sgnl(t)
            lapse_x(t)
        act(at("y0a"), at("Y", 0, W, 16), AF.Identity, bias=12582912.0)
        act(at("y0b"), at("y0a"), AF.Identity, bias=-12582912.0)
        gather("S", at("Tf"), at("Lf"), at("P16", 16 * c, 16 * c + 16))
        x1, xs, R = at("x1_%d" % (t % 2)), at("xs%d" % t), at("SCN", 15, W, 16)
        ts(at("mi"), R, -0.5, None, A.add)
        tt(x1, at("mi"), x0col(t), A.min)
        mm(at("pV", 0, K), at("Bn"), x1, False, True)
        mm(at("pH", 0, K), at("Blk"), at("y0b"), True, True)
        tt(at("mx"), x1, at("pV", 0, K), A.max)
        tt(xs, at("mx"), at("pB", 0, K), A.min)
        d = 1 + t % (N - 1)
        nxt, prv = T.cores[(rank + d) % N], T.cores[(rank - d) % N]
        arr, loc = "arr%d" % t, "loc%d" % t
        waits("G", loc, [xs], [])
        rid, pid, _ = topo.addr(nxt)
        g.remote_dma(out_ap=T["land%d" % t][:], in_ap=xs[0], remote_sem=T.sem[arr], local_sem=T.sem[loc],
                     pid=pid, routing_id=rid, dma_engine_mask=topo.mask(core, nxt))
        note("G", loc, loc, len(topo.engines(core, nxt)), [xs], [])
        note(None, arr, arr, len(topo.engines(prv, core)), [], [at("land%d" % t)])
        if not late:
            if t > 0:
                xbput(o - K, "xs%d" % (t - 1))
                xbput(told(t - 1), "land%d" % (t - 1))
            fargather(t, 0)
            if t > 0:
                sgnl(t - 1)
                schain_pe(t - 1)
            sgnd(t)
            fargather(t, 1)
        else:
            sgnd(t)
        if t >= 3:
            xbput(o, "xs%d" % t)
            if t < RO - 1:
                xbput(told(t), "land%d" % t)
        if t < RO - 1:
            tt(at("Z", o, o + K), xs, at("pJ", 0, K), A.add)
        cp(at("hi"), at("pH", 0, K))
        ts(at("h15"), at("hi"), 15, None, A.bitwise_and)
        ts(at("mask"), at("h15"), at("kcf"), None, A.is_equal)
        qo, po = at("Q16", 16 * c, 16 * c + 16), at("P16", 16 * c, 16 * c + 16)
        emit("V", lambda: g.vector.tensor_tensor(out=T.mLQ[:], in0=T.Lf[:].indirect(qo[0]), in1=T.mask[:], op=A.mult), [at("mLQ")], [at("Lf"), qo, at("mask")])
        group(at("pH", K, 2 * K), [(at("Imf"), at("Tf")), (at("Blkf"), at("mLQ"))])
        tt(at("w"), at("pV", 0, K), at("THR", t, t + K), A.is_gt)
        tt(at("Fm%d" % (t % 2)), R, x0col(t), A.min)
        if t == 0:
            consts2()
        if 0 < t < 4:
            schain_v(t - 1)
        tt(at("q"), at("pH", K, 2 * K), at("w"), A.mult)
        emit("V", lambda: g.vector.tensor_tensor(out=T.Lf[:].indirect(po[0]), in0=T.q[:], in1=T.Tf[:], op=A.add), [at("Lf")], [at("q"), at("Tf"), po])
        if t < RO - 1:
            tgather(t + 1)
            n = told(t)
            tt(at("Z", n, n + K), at("land%d" % t), at("pJ", K, 2 * K), A.add)
        if t < 3:
            farstart(t)
            bg.extend(farops(t))
        if t == 2:
            for lo, hi in ((1280, 1792), (2560, 3328), (3840, 4096)):
                dma("Y", T.yx[:, lo:hi], at("Xb", lo, hi))
    dma("Y", T.yl[:], at("Lf"))
    for lo, hi in ((0, 1280), (1792, 2560), (3584, 3840)):
        dma("Y", T.yx[:, lo:hi], at("Xb", lo, hi))
    schain_pe(RO - 1)
    n = told(RO - 1)
    xbput(n, "land%d" % (RO - 1))
    dma("Y", T.yx[:, n:n + K], at("Xb", n, n + K))
    schain_v(RO - 1)
    for s, n in count.items():
        if n and clk["Y"].get(s, 0) < n:
            g.sync.wait_ge(T.sem[s], n)
